import numpy as np
import ml_dtypes


def mxq(x, axis, fmt="e4m3"):
    dtype, down = {"e4m3": (ml_dtypes.float8_e4m3fn, 7), "e5m2": (ml_dtypes.float8_e5m2, 14)}[fmt]
    v = np.moveaxis(np.asarray(x, np.float32).astype(ml_dtypes.bfloat16).astype(np.float64), axis, -1)
    blocks = v.reshape(v.shape[:-1] + (-1, 32))
    amax = np.abs(blocks).max(-1, keepdims=True)
    byte = np.maximum(np.where(amax > 0, np.frexp(amax)[1] - 1 + 127, 0) - down, 1)
    scale = np.exp2(byte - 127.0)
    codes = (blocks / scale).astype(np.float32).astype(dtype).astype(np.float64)
    return np.moveaxis((codes * scale).reshape(v.shape), -1, axis)


WIDE = False


def mx_kscale(k):
    if not WIDE:
        return np.ones(k)
    levels = np.array([10, -10, 5, -5, 0])
    if k % 512:
        return np.exp2(np.random.permutation(np.resize(levels, k // 32))).repeat(32)
    a = np.empty((k // 512, 16))
    for p in range(k // 512):
        a[p, :8] = np.random.permutation(np.resize(levels, 8))
        for g in range(8):
            far = levels[np.abs(levels - a[p, g]) >= 10]
            a[p, g + 8] = far[np.random.randint(len(far))]
    return np.exp2(a.ravel()).repeat(32)


def f64(x):
    return np.asarray(x).astype(np.float64)


def striped(idx):
    return np.tile(idx.reshape(-1, 16).T, (8, 1)).astype(np.uint16)


def unstriped(offs):
    return offs[:16].T.reshape(-1).astype(np.int64)


def striped8(idx):
    return np.concatenate([x.reshape(-1, 16).T for x in idx]).astype(np.uint16)


def runs(offs, k):
    lists = np.stack([offs[16 * r : 16 * r + 16].T.reshape(-1) for r in range(8)]).astype(np.int64)
    return lists[np.arange(k) % 512 // 64]


def pack_weight(w):
    k, n = w.shape
    w = f64(np.asarray(w, np.float32).astype(ml_dtypes.bfloat16)).reshape(k // 32, 32, n)
    amax = np.abs(w).max(1)
    byte = np.clip(np.where(amax > 0, np.frexp(amax)[1] - 1 + 127 - 7, 1), 1, 254)
    scaled = (w * np.exp2(127.0 - byte)[:, None, :]).reshape(k, n).astype(np.float32)
    words = np.ascontiguousarray(scaled.reshape(k // 512, 128, 4, n).transpose(0, 1, 3, 2)).astype(ml_dtypes.float8_e4m3fn).view(np.uint8)
    return words, np.ascontiguousarray(byte.astype(np.uint8).reshape(k // 512, 16, n))


def unpack_weight(words, scales):
    g, p, n, _ = words.shape
    vals = np.ascontiguousarray(words).view(ml_dtypes.float8_e4m3fn).astype(np.float64) * np.repeat(np.exp2(scales.astype(np.float64) - 127.0), 8, axis=1)[..., None]
    return vals.transpose(0, 1, 3, 2).reshape(g * 512, n)


def sigmoid(v):
    return 1.0 / (1.0 + np.exp(-np.maximum(v, -700.0)))


K, T, S, G, H, W = 512, 1024, 512, 2048, 512, 256


def setup_inputs():
    n = np.random.standard_normal
    s = mx_kscale(K)[:, None]
    packed_xT = pack_weight(n((K, T)) * s)
    packed_dT = pack_weight(n((K, G)) / s)
    perm = np.stack([np.random.permutation(S) for _ in range(8)])
    perm2 = np.stack([np.random.permutation(S) for _ in range(8)])
    perm3 = np.stack([np.random.permutation(S) for _ in range(8)])
    perm4 = np.stack([np.random.permutation(S) for _ in range(8)])
    return {
        "x_words": packed_xT[0],
        "x_scales": packed_xT[1],
        "d_words": packed_dT[0],
        "d_scales": packed_dT[1],
        "gs": (np.random.uniform(0.5, 1.5, (K, 1)) * s).astype(np.float32),
        "sl": np.random.uniform(1.0, 2.0, (H, 1)).astype(np.float32),
        "th": (0.5 * n((H, 1))).astype(np.float32),
        "offs": striped8(np.random.randint(0, T, (8, S))),
        "ka": striped8(np.random.randint(0, G, (8, H))),
        "kb": striped8(np.random.randint(0, G, (8, H))),
        "n1": striped8(perm[:, :W]),
        "n2": striped8(perm[:, W:]),
        "n3": striped8(perm2[:, :W]),
        "n4": striped8(perm2[:, W:]),
        "k1": striped8(np.random.randint(0, G, (8, H))),
        "k2": striped8(np.random.randint(0, G, (8, H))),
        "two": striped(np.random.permutation(T)[:S]),
        "n5": striped8(np.stack([np.random.permutation(S) for _ in range(8)])),
        "n6": striped8(perm3[:, :W]),
        "n7": striped8(perm3[:, W:]),
        "n8": striped8(perm4[:, :W]),
        "n9": striped8(perm4[:, W:]),
    }


def reference(x_words, x_scales, d_words, d_scales, gs, sl, th, offs, ka, kb, n1, n2, n3, n4, k1, k2, two, n5, n6, n7, n8, n9):
    d_k1 = unpack_weight(d_words, d_scales)[np.arange(K)[:, None], runs(k1, K)]
    d_ka = unpack_weight(d_words, d_scales)[np.arange(K)[:, None], runs(ka, K)]
    xq = unpack_weight(x_words, x_scales)[np.arange(K)[:, None], runs(offs, K)]
    d_kb = unpack_weight(d_words, d_scales)[np.arange(K)[:, None], runs(kb, K)]
    h = 0.0625 * (d_ka.T @ xq + d_kb.T @ xq)
    pa = h[np.arange(H)[:, None], runs(n1, H)]
    pb = h[np.arange(H)[:, None], runs(n2, H)]
    rb = pa - pb
    ra = np.maximum(pa, pb)
    ua = np.zeros((H, S))
    ua[np.arange(H)[:, None], runs(n3, H)] = ra
    ub = ua.copy()
    ub[np.arange(H)[:, None], runs(n4, H)] = rb
    z = f64(gs) * ub
    d_k2 = unpack_weight(d_words, d_scales)[np.arange(K)[:, None], runs(k2, K)]
    x_two = unpack_weight(x_words, x_scales)[:, unstriped(two)]
    h2 = 0.0625 * ((d_k1.T @ mxq(z, 0, "e4m3") + d_k2.T @ x_two))
    sg = sigmoid(f64(sl) * (h2[np.arange(H)[:, None], runs(n5, H)] - f64(th)))
    st = h2 * sg
    pa2 = st[np.arange(H)[:, None], runs(n6, H)]
    pb2 = st[np.arange(H)[:, None], runs(n7, H)]
    rb2 = pa2 - pb2
    ra2 = np.maximum(pa2, pb2)
    ua2 = np.zeros((H, S))
    ua2[np.arange(H)[:, None], runs(n8, H)] = ra2
    out = ua2.copy()
    out[np.arange(H)[:, None], runs(n9, H)] = rb2
    return out

@@ -1,0 +1,207 @@
+from contextlib import ExitStack
+
+import concourse.mybir as mybir
+
+F32 = mybir.dt.float32
+BF16 = mybir.dt.bfloat16
+I32 = mybir.dt.int32
+U32 = mybir.dt.uint32
+U16 = mybir.dt.uint16
+U8 = mybir.dt.uint8
+FP8X4 = mybir.dt.float8_e4m3fn_x4
+ACT = mybir.ActivationFunctionType
+ALU = mybir.AluOpType
+
+P = 128
+PACK = 4
+S = 512
+W = 256
+FLOPS = 4 * 2 * 512 * 512 * 512
+
+
+def tile_picked_ahzmtcpmxecpx_none_p_kernel(
+    tc, x_words, x_scales, d_words, d_scales, gs, sl, th, offs, ka, kb, n1, n2, n3, n4, k1, k2, two, n5, n6, n7, n8, n9, out
+):
+    nc = tc.nc
+    with ExitStack() as ctx:
+        held = ctx.enter_context(tc.tile_pool(name="held", bufs=1))
+        work = ctx.enter_context(tc.tile_pool(name="work", bufs=1))
+        psum = ctx.enter_context(tc.psum_pool(name="psum", bufs=1))
+
+        lists = {}
+        for name, src in (
+            ("offs", offs), ("ka", ka), ("kb", kb), ("n1", n1), ("n2", n2), ("two", two), ("k2", k2), ("k1", k1),
+            ("n4", n4), ("n3", n3), ("n5", n5), ("n6", n6), ("n7", n7), ("n9", n9), ("n8", n8),
+        ):
+            lists[name] = held.tile(list(src.shape), U16, name="list_" + name)
+            nc.sync.dma_start(lists[name][:], src)
+
+        def load_scale_window(name, src):
+            cols = src.shape[2]
+            window = held.tile([P, cols], U8, name=name, align_bytes=64)
+            rows = src[0].bitcast(I32)
+            nc.scalar.dma_start(window[:].bitcast(I32), rows.unsqueeze(1).broadcast_to([16, 8, cols // 4]))
+            return window
+
+        def load_word_window(name, src):
+            cols = src.shape[2]
+            window = held.tile([P, cols], U32, name=name, align_bytes=64)
+            nc.scalar.dma_start(window[:].bitcast(I32), src[0].rearrange("p n t -> p (n t)").bitcast(I32))
+            return window
+
+        xs = load_scale_window("xs", x_scales)
+        ds = load_scale_window("ds", d_scales)
+        xw = load_word_window("xw", x_words)
+        dw = load_word_window("dw", d_words)
+
+        cols4 = {}
+        for name, src in (("gs", gs), ("sl", sl), ("th", th)):
+            cols4[name] = held.tile([P, PACK], F32, name="row_" + name)
+            nc.sync.dma_start(cols4[name][:], src.rearrange("(p t) o -> p (t o)", t=PACK))
+
+        planes = []
+        for stage in range(2):
+            plane = held.tile([P, 3, S], U8, name="planes%d" % stage, align_bytes=64)
+            nc.vector.memset(plane[:].rearrange("p l c -> p (l c)").bitcast(I32), 0)
+            planes.append(plane)
+
+        def gather_scales(stage, tag, x_list, d_lists):
+            picked = work.tile([P, 3, S], U8, name="picked_b%d" % stage, tag=tag, align_bytes=64)
+            nc.vector.tensor_copy(picked[:, 0, :], xs[:].indirect(lists[x_list][:]))
+            for l, name in enumerate(d_lists):
+                nc.vector.tensor_copy(picked[:, 1 + l, :], ds[:].indirect(lists[name][:]))
+            dealt = work.tile([P, 2, S], U8, name="dealt_b%d" % stage, align_bytes=64)
+            nc.vector.tensor_copy(
+                dealt[:].rearrange("p l (t a m) -> p l a t m", t=PACK, m=16),
+                picked[:, 1:3, :].rearrange("p l (a m t) -> p l a t m", t=PACK, m=16),
+            )
+            flat = planes[stage][:].rearrange("p l c -> p (l c)").bitcast(I32)
+            x_src = picked[:].rearrange("p l c -> p (l c)").bitcast(I32)
+            d_src = dealt[:].rearrange("p l c -> p (l c)").bitcast(I32)
+            for i in range(4):
+                nc.sync.dma_start(flat[i:P:32, 0 : S // 4], x_src[8 * i : P : 32, 0 : S // 4])
+            for i in range(4):
+                nc.sync.dma_start(flat[i:P:32, S // 4 : 3 * S // 4], d_src[8 * i : P : 32, :])
+
+        def gather_words(window, name, tag):
+            picked = work.tile([P, S], U32, name="picked_" + name, tag=tag, align_bytes=64)
+            nc.vector.tensor_copy(picked[:], window[:].indirect(lists[name][:]))
+            return picked
+
+        def deal_words(picked, name):
+            dealt = work.tile([P, S], U32, name="dealt_" + name, align_bytes=64)
+            nc.vector.tensor_copy(
+                dealt[:].bitcast(I32).rearrange("p (t a m) -> p a t m", t=PACK, m=4),
+                picked[:].bitcast(I32).rearrange("p (a m t) -> p a t m", t=PACK, m=4),
+            )
+            return dealt
+
+        def mx_pass(bank, t, lhs, lhs_plane, rhs, rhs_plane, first):
+            cols = slice(t * P, (t + 1) * P)
+            nc.tensor.matmul_mx(
+                out=bank[:], lhsT=lhs[:, cols].bitcast(FP8X4), lhsT_scale=lhs_plane[:, cols],
+                rhs=rhs[:].bitcast(FP8X4), rhs_scale=rhs_plane, start=first, stop=not first,
+            )
+
+        def fetch_pairs(window, t, stage, first, second):
+            pair = work.tile([P, 2, W], F32, name="pair%d_%d" % (stage, t))
+            nc.scalar.activation(pair[:, 0, :], window[:].indirect(lists[first][:]), ACT.Copy)
+            if stage == 1 and t == 0:
+                nc.vector.tensor_scalar(pair[:, 1, :], window[:].indirect(lists[second][:]), -1.0, 0.0, ALU.mult, ALU.add)
+            else:
+                nc.scalar.activation(pair[:, 1, :], window[:].indirect(lists[second][:]), ACT.Copy, scale=-1.0)
+            return pair
+
+        def take_larger(pair, name, tag):
+            larger = work.tile([P, W], F32, name=name, tag=tag, align_bytes=64)
+            nc.vector.scalar_tensor_tensor(larger[:], pair[:, 1, :], -1.0, pair[:, 0, :], ALU.mult, ALU.max)
+            return larger
+
+        def place_difference(pair, name, to_difference):
+            placed = work.tile([P, S], F32, name=name)
+            nc.vector.tensor_tensor(placed[:].indirect(lists[to_difference][:]), pair[:, 0, :], pair[:, 1, :], ALU.add)
+            return placed
+
+        def place_larger(placed, larger, to_larger):
+            nc.vector.tensor_copy(placed[:].indirect(lists[to_larger][:]), larger[:])
+
+        gather_scales(0, "picked_b0", "offs", ("ka", "kb"))
+        xq = gather_words(xw, "offs", "picked_offs")
+        da = deal_words(gather_words(dw, "ka", "picked_ka"), "ka")
+        db = deal_words(gather_words(dw, "kb", "picked_kb"), "kb")
+
+        banks = [psum.tile([P, S], F32, name="bank%d" % b) for b in range(2 * PACK)]
+        pairs = []
+        for t in range(PACK):
+            mx_pass(banks[t], t, da, planes[0][:, 1, :], xq, planes[0][:, 0, :], True)
+            mx_pass(banks[t], t, db, planes[0][:, 2, :], xq, planes[0][:, 0, :], False)
+            h = work.tile([P, S], F32, name="h%d" % t)
+            nc.scalar.activation(h[:], banks[t][:], ACT.Copy, scale=0.0625)
+            pairs.append(fetch_pairs(h, t, 0, "n1", "n2"))
+
+        gather_scales(1, "picked_kb", "two", ("k1", "k2"))
+        x2 = gather_words(xw, "two", "picked_ka")
+        d2 = deal_words(gather_words(dw, "k2", "picked_k2"), "k2")
+        for t in range(PACK):
+            mx_pass(banks[PACK + t], t, d2, planes[1][:, 2, :], x2, planes[1][:, 0, :], True)
+
+        bias = held.tile([P, PACK], F32, name="bias")
+        nc.vector.scalar_tensor_tensor(bias[:], cols4["sl"][:], -1.0, cols4["th"][:], ALU.mult, ALU.mult)
+
+        z_halves = [work.tile([P, W, PACK], BF16, name="z%d" % half, align_bytes=64) for half in range(2)]
+        for t in range(PACK):
+            larger = take_larger(pairs[t], "larger0_%d" % t, "larger0_%d" % t)
+            ub = place_difference(pairs[t], "ub%d" % t, "n4")
+            place_larger(ub, larger, "n3")
+            for half in range(2):
+                nc.scalar.activation(
+                    z_halves[half][:, :, t], ub[:, half * W : (half + 1) * W], ACT.Copy, scale=cols4["gs"][:, t : t + 1]
+                )
+
+        d1 = deal_words(gather_words(dw, "k1", "larger0_3"), "k1")
+        z_codes = work.tile([P, S], U32, name="z_codes", align_bytes=64)
+        z_plane = work.tile([P, S], U8, name="z_plane", align_bytes=64)
+        for half in range(2):
+            cols = slice(half * W, (half + 1) * W)
+            nc.vector.quantize_mx(
+                out=z_codes[:, cols].bitcast(FP8X4), scales=z_plane[:, cols], in_=z_halves[half][:].rearrange("p c t -> p (c t)")
+            )
+
+        def gate_rows(t):
+            bank = banks[PACK + t]
+            rows_t = slice(t * P, (t + 1) * P)
+            pieces = 2 if t == 0 else 1
+            width = S // pieces
+            for piece in range(pieces):
+                cols = slice(piece * width, (piece + 1) * width)
+                nc.tensor.matmul_mx(
+                    out=bank[:, cols], lhsT=d1[:, rows_t].bitcast(FP8X4), lhsT_scale=planes[1][:, 1, rows_t],
+                    rhs=z_codes[:, cols].bitcast(FP8X4), rhs_scale=z_plane[:, cols], start=False, stop=piece == pieces - 1,
+                )
+            h2 = work.tile([P, S], F32, name="h2_%d" % t, tag="h2_%d" % (t % 2))
+            if t < 2:
+                nc.vector.tensor_scalar(h2[:], bank[:], 0.0625, None, ALU.mult)
+            else:
+                nc.scalar.activation(h2[:], bank[:], ACT.Copy, scale=0.0625)
+            sg = work.tile([P, S], F32, name="sg%d" % t, tag="sg%d" % t, align_bytes=64)
+            for half in range(2):
+                nc.scalar.activation(
+                    sg[:, half * W : (half + 1) * W], h2[:].indirect(lists["n5"][:, half * 16 : (half + 1) * 16]), ACT.Sigmoid,
+                    scale=cols4["sl"][:, t : t + 1], bias=bias[:, t : t + 1],
+                )
+            st = work.tile([P, S], F32, name="st%d" % t)
+            for piece in range(pieces):
+                cols = slice(piece * width, (piece + 1) * width)
+                nc.vector.tensor_tensor(st[:, cols], h2[:, cols], sg[:, cols], ALU.mult)
+            return st
+
+        rows = out.rearrange("(p t) c -> p t c", t=PACK)
+        st = gate_rows(0)
+        for t in range(PACK):
+            pair = fetch_pairs(st, t, 1, "n6", "n7")
+            result = place_difference(pair, "result%d" % t, "n9")
+            if t + 1 < PACK:
+                st = gate_rows(t + 1)
+            larger = take_larger(pair, "larger1_%d" % t, "sg%d" % ((t + 1) % PACK))
+            place_larger(result, larger, "n8")
+            nc.sync.dma_start(rows[:, t, :], result[:])

@@ -54,10 +54,8 @@ def tile_picked_ahzmtcpmxecpx_none_p_kernel(
         xw = load_word_window("xw", x_words)
         dw = load_word_window("dw", d_words)
 
-        cols4 = {}
-        for name, src in (("gs", gs), ("sl", sl), ("th", th)):
-            cols4[name] = held.tile([P, PACK], F32, name="row_" + name)
-            nc.sync.dma_start(cols4[name][:], src.rearrange("(p t) o -> p (t o)", t=PACK))
+        cols4 = {"gs": held.tile([P, PACK], F32, name="row_gs")}
+        nc.sync.dma_start(cols4["gs"][:], gs.rearrange("(p t) o -> p (t o)", t=PACK))
 
         planes = []
         for stage in range(2):
@@ -70,11 +68,17 @@ def tile_picked_ahzmtcpmxecpx_none_p_kernel(
             nc.vector.tensor_copy(picked[:, 0, :], xs[:].indirect(lists[x_list][:]))
             for l, name in enumerate(d_lists):
                 nc.vector.tensor_copy(picked[:, 1 + l, :], ds[:].indirect(lists[name][:]))
-            dealt = work.tile([P, 2, S], U8, name="dealt_b%d" % stage, align_bytes=64)
-            nc.vector.tensor_copy(
-                dealt[:].rearrange("p l (t a m) -> p l a t m", t=PACK, m=16),
-                picked[:, 1:3, :].rearrange("p l (a m t) -> p l a t m", t=PACK, m=16),
-            )
+            dealt = work.tile([P, 2, S], U8, name="dealt_b%d" % stage, tag="dealt_b%d" % stage, align_bytes=64)
+            if stage == 0:
+                nc.vector.tensor_copy(
+                    dealt[:].rearrange("p l (t a m) -> p l a t m", t=PACK, m=16),
+                    picked[:, 1:3, :].rearrange("p l (a m t) -> p l a t m", t=PACK, m=16),
+                )
+            else:
+                nc.vector.tensor_copy(
+                    dealt[:].bitcast(I32).rearrange("p l (t g b) -> p l t g b", t=PACK, b=2),
+                    picked[:, 1:3, :].bitcast(I32).rearrange("p l (g t b) -> p l t g b", t=PACK, b=2),
+                )
             flat = planes[stage][:].rearrange("p l c -> p (l c)").bitcast(I32)
             x_src = picked[:].rearrange("p l c -> p (l c)").bitcast(I32)
             d_src = dealt[:].rearrange("p l c -> p (l c)").bitcast(I32)
@@ -90,10 +94,16 @@ def tile_picked_ahzmtcpmxecpx_none_p_kernel(
 
         def deal_words(picked, name):
             dealt = work.tile([P, S], U32, name="dealt_" + name, align_bytes=64)
-            nc.vector.tensor_copy(
-                dealt[:].bitcast(I32).rearrange("p (t a m) -> p a t m", t=PACK, m=4),
-                picked[:].bitcast(I32).rearrange("p (a m t) -> p a t m", t=PACK, m=4),
-            )
+            if name in ("ka", "kb"):
+                nc.vector.tensor_copy(
+                    dealt[:].bitcast(I32).rearrange("p (t a m) -> p a t m", t=PACK, m=4),
+                    picked[:].bitcast(I32).rearrange("p (a m t) -> p a t m", t=PACK, m=4),
+                )
+            else:
+                nc.vector.tensor_copy(
+                    dealt[:].bitcast(I32).rearrange("p (t g b) -> p t g b", t=PACK, b=8),
+                    picked[:].bitcast(I32).rearrange("p (g t b) -> p t g b", t=PACK, b=8),
+                )
             return dealt
 
         def mx_pass(bank, t, lhs, lhs_plane, rhs, rhs_plane, first):
@@ -104,7 +114,7 @@ def tile_picked_ahzmtcpmxecpx_none_p_kernel(
             )
 
         def fetch_pairs(window, t, stage, first, second):
-            pair = work.tile([P, 2, W], F32, name="pair%d_%d" % (stage, t))
+            pair = work.tile([P, 2, W], F32, name="pair%d_%d" % (stage, t), tag="pair%d_%d" % (stage, t))
             nc.scalar.activation(pair[:, 0, :], window[:].indirect(lists[first][:]), ACT.Copy)
             if stage == 1 and t == 0:
                 nc.vector.tensor_scalar(pair[:, 1, :], window[:].indirect(lists[second][:]), -1.0, 0.0, ALU.mult, ALU.add)
@@ -117,8 +127,8 @@ def tile_picked_ahzmtcpmxecpx_none_p_kernel(
             nc.vector.scalar_tensor_tensor(larger[:], pair[:, 1, :], -1.0, pair[:, 0, :], ALU.mult, ALU.max)
             return larger
 
-        def place_difference(pair, name, to_difference):
-            placed = work.tile([P, S], F32, name=name)
+        def place_difference(pair, name, tag, to_difference):
+            placed = work.tile([P, S], F32, name=name, tag=tag, align_bytes=64)
             nc.vector.tensor_tensor(placed[:].indirect(lists[to_difference][:]), pair[:, 0, :], pair[:, 1, :], ALU.add)
             return placed
 
@@ -145,13 +155,18 @@ def tile_picked_ahzmtcpmxecpx_none_p_kernel(
         for t in range(PACK):
             mx_pass(banks[PACK + t], t, d2, planes[1][:, 2, :], x2, planes[1][:, 0, :], True)
 
+        for name, src, tag in (("sl", sl, "dealt_b0"), ("th", th, "picked_b0")):
+            cols4[name] = work.tile([P, PACK, 8], F32, name="row_" + name, tag=tag, align_bytes=64)
+            for t in range(PACK):
+                with nc.allow_non_contiguous_dma(reason="one value a row"):
+                    nc.sync.dma_start(cols4[name][:, t, 0:1], src.rearrange("(g t b) o -> t g b o", t=PACK, b=8)[t])
         bias = held.tile([P, PACK], F32, name="bias")
-        nc.vector.scalar_tensor_tensor(bias[:], cols4["sl"][:], -1.0, cols4["th"][:], ALU.mult, ALU.mult)
+        nc.vector.scalar_tensor_tensor(bias[:], cols4["sl"][:, :, 0], -1.0, cols4["th"][:, :, 0], ALU.mult, ALU.mult)
 
         z_halves = [work.tile([P, W, PACK], BF16, name="z%d" % half, align_bytes=64) for half in range(2)]
         for t in range(PACK):
             larger = take_larger(pairs[t], "larger0_%d" % t, "larger0_%d" % t)
-            ub = place_difference(pairs[t], "ub%d" % t, "n4")
+            ub = place_difference(pairs[t], "ub%d" % t, "ub%d" % t, "n4")
             place_larger(ub, larger, "n3")
             for half in range(2):
                 nc.scalar.activation(
@@ -187,21 +202,24 @@ def tile_picked_ahzmtcpmxecpx_none_p_kernel(
             for half in range(2):
                 nc.scalar.activation(
                     sg[:, half * W : (half + 1) * W], h2[:].indirect(lists["n5"][:, half * 16 : (half + 1) * 16]), ACT.Sigmoid,
-                    scale=cols4["sl"][:, t : t + 1], bias=bias[:, t : t + 1],
+                    scale=cols4["sl"][:, t, 0:1], bias=bias[:, t : t + 1],
                 )
-            st = work.tile([P, S], F32, name="st%d" % t)
+            st = work.tile([P, S], F32, name="st%d" % t, tag="st%d" % t if t < 2 else "pair1_%d" % (t - 2))
+            engine = nc.vector if t < 2 else nc.gpsimd
             for piece in range(pieces):
                 cols = slice(piece * width, (piece + 1) * width)
-                nc.vector.tensor_tensor(st[:, cols], h2[:, cols], sg[:, cols], ALU.mult)
+                engine.tensor_tensor(st[:, cols], h2[:, cols], sg[:, cols], ALU.mult)
             return st
 
-        rows = out.rearrange("(p t) c -> p t c", t=PACK)
-        st = gate_rows(0)
+        rows = out.rearrange("(g t b) c -> t g b c", t=PACK, b=8)
+        gated = [gate_rows(0)]
         for t in range(PACK):
-            pair = fetch_pairs(st, t, 1, "n6", "n7")
-            result = place_difference(pair, "result%d" % t, "n9")
-            if t + 1 < PACK:
-                st = gate_rows(t + 1)
-            larger = take_larger(pair, "larger1_%d" % t, "sg%d" % ((t + 1) % PACK))
+            pair = fetch_pairs(gated[t], t, 1, "n6", "n7")
+            larger = take_larger(pair, "larger1_%d" % t, "larger1_%d" % t)
+            if t == 0:
+                gated.append(gate_rows(1))
+            result = place_difference(pair, "result%d" % t, "sg1" if t == 0 else "result%d" % t, "n9")
+            if t + 2 < PACK:
+                gated.append(gate_rows(t + 2))
             place_larger(result, larger, "n8")
-            nc.sync.dma_start(rows[:, t, :], result[:])
+            nc.sync.dma_start(rows[t], result[:])

@@ -13,9 +13,14 @@ ACT = mybir.ActivationFunctionType
 ALU = mybir.AluOpType
 
 P = 128
-PACK = 4
+TILES = 4
 S = 512
 W = 256
+HALF_LIST = W // 16
+RUN = 8
+SCALE_ROWS = 16
+SIXTEENTH = 0.0625
+HALVES = (slice(0, W), slice(W, S))
 FLOPS = 4 * 2 * 512 * 512 * 512
 
 
@@ -39,187 +44,188 @@ def tile_picked_ahzmtcpmxecpx_none_p_kernel(
         def load_scale_window(name, src):
             cols = src.shape[2]
             window = held.tile([P, cols], U8, name=name, align_bytes=64)
-            rows = src[0].bitcast(I32)
-            nc.scalar.dma_start(window[:].bitcast(I32), rows.unsqueeze(1).broadcast_to([16, 8, cols // 4]))
+            scale_rows = src[0].bitcast(I32).unsqueeze(1).broadcast_to([SCALE_ROWS, P // SCALE_ROWS, cols // 4])
+            nc.scalar.dma_start(window[:].bitcast(I32), scale_rows)
             return window
 
         def load_word_window(name, src):
-            cols = src.shape[2]
-            window = held.tile([P, cols], U32, name=name, align_bytes=64)
+            window = held.tile([P, src.shape[2]], U32, name=name, align_bytes=64)
             nc.scalar.dma_start(window[:].bitcast(I32), src[0].rearrange("p n t -> p (n t)").bitcast(I32))
             return window
 
-        xs = load_scale_window("xs", x_scales)
-        ds = load_scale_window("ds", d_scales)
-        xw = load_word_window("xw", x_words)
-        dw = load_word_window("dw", d_words)
+        x_scale_window = load_scale_window("x_scale_window", x_scales)
+        d_scale_window = load_scale_window("d_scale_window", d_scales)
+        x_word_window = load_word_window("x_word_window", x_words)
+        d_word_window = load_word_window("d_word_window", d_words)
 
-        cols4 = {"gs": held.tile([P, PACK], F32, name="row_gs")}
-        nc.sync.dma_start(cols4["gs"][:], gs.rearrange("(p t) o -> p (t o)", t=PACK))
+        gains = held.tile([P, TILES], F32, name="gains")
+        nc.sync.dma_start(gains[:], gs.rearrange("(p t) o -> p (t o)", t=TILES))
 
         planes = []
-        for stage in range(2):
-            plane = held.tile([P, 3, S], U8, name="planes%d" % stage, align_bytes=64)
+        for layer in range(2):
+            plane = held.tile([P, 3, S], U8, name="planes%d" % layer, align_bytes=64)
             nc.vector.memset(plane[:].rearrange("p l c -> p (l c)").bitcast(I32), 0)
             planes.append(plane)
 
-        def gather_scales(stage, tag, x_list, d_lists):
-            picked = work.tile([P, 3, S], U8, name="picked_b%d" % stage, tag=tag, align_bytes=64)
-            nc.vector.tensor_copy(picked[:, 0, :], xs[:].indirect(lists[x_list][:]))
-            for l, name in enumerate(d_lists):
-                nc.vector.tensor_copy(picked[:, 1 + l, :], ds[:].indirect(lists[name][:]))
-            dealt = work.tile([P, 2, S], U8, name="dealt_b%d" % stage, tag="dealt_b%d" % stage, align_bytes=64)
-            if stage == 0:
-                nc.vector.tensor_copy(
-                    dealt[:].rearrange("p l (t a m) -> p l a t m", t=PACK, m=16),
-                    picked[:, 1:3, :].rearrange("p l (a m t) -> p l a t m", t=PACK, m=16),
-                )
-            else:
-                nc.vector.tensor_copy(
-                    dealt[:].bitcast(I32).rearrange("p l (t g b) -> p l t g b", t=PACK, b=2),
-                    picked[:, 1:3, :].bitcast(I32).rearrange("p l (g t b) -> p l t g b", t=PACK, b=2),
-                )
-            flat = planes[stage][:].rearrange("p l c -> p (l c)").bitcast(I32)
-            x_src = picked[:].rearrange("p l c -> p (l c)").bitcast(I32)
-            d_src = dealt[:].rearrange("p l c -> p (l c)").bitcast(I32)
+        def deal_bytes_by_fours(dealt, picked):
+            nc.vector.tensor_copy(
+                dealt.rearrange("p l (t a m) -> p l a t m", t=TILES, m=16),
+                picked.rearrange("p l (a m t) -> p l a t m", t=TILES, m=16),
+            )
+
+        def deal_bytes_by_runs(dealt, picked):
+            nc.vector.tensor_copy(
+                dealt.bitcast(I32).rearrange("p l (t g b) -> p l t g b", t=TILES, b=RUN // 4),
+                picked.bitcast(I32).rearrange("p l (g t b) -> p l t g b", t=TILES, b=RUN // 4),
+            )
+
+        def gather_scales(layer, tag, x_list, d_lists, deal):
+            picked = work.tile([P, 3, S], U8, name="picked_bytes%d" % layer, tag=tag, align_bytes=64)
+            nc.vector.tensor_copy(picked[:, 0, :], x_scale_window[:].indirect(lists[x_list][:]))
+            for slot, name in enumerate(d_lists):
+                nc.vector.tensor_copy(picked[:, 1 + slot, :], d_scale_window[:].indirect(lists[name][:]))
+            dealt = work.tile([P, 2, S], U8, name="dealt_bytes%d" % layer, tag="dealt_bytes%d" % layer, align_bytes=64)
+            deal(dealt[:], picked[:, 1:3, :])
+            target = planes[layer][:].rearrange("p l c -> p (l c)").bitcast(I32)
+            x_source = picked[:].rearrange("p l c -> p (l c)").bitcast(I32)
+            d_source = dealt[:].rearrange("p l c -> p (l c)").bitcast(I32)
             for i in range(4):
-                nc.sync.dma_start(flat[i:P:32, 0 : S // 4], x_src[8 * i : P : 32, 0 : S // 4])
+                nc.sync.dma_start(target[i:P:32, 0 : S // 4], x_source[8 * i : P : 32, 0 : S // 4])
             for i in range(4):
-                nc.sync.dma_start(flat[i:P:32, S // 4 : 3 * S // 4], d_src[8 * i : P : 32, :])
+                nc.sync.dma_start(target[i:P:32, S // 4 : 3 * S // 4], d_source[8 * i : P : 32, :])
 
         def gather_words(window, name, tag):
             picked = work.tile([P, S], U32, name="picked_" + name, tag=tag, align_bytes=64)
             nc.vector.tensor_copy(picked[:], window[:].indirect(lists[name][:]))
             return picked
 
-        def deal_words(picked, name):
+        def deal_words_by_fours(picked, name):
             dealt = work.tile([P, S], U32, name="dealt_" + name, align_bytes=64)
-            if name in ("ka", "kb"):
-                nc.vector.tensor_copy(
-                    dealt[:].bitcast(I32).rearrange("p (t a m) -> p a t m", t=PACK, m=4),
-                    picked[:].bitcast(I32).rearrange("p (a m t) -> p a t m", t=PACK, m=4),
-                )
-            else:
-                nc.vector.tensor_copy(
-                    dealt[:].bitcast(I32).rearrange("p (t g b) -> p t g b", t=PACK, b=8),
-                    picked[:].bitcast(I32).rearrange("p (g t b) -> p t g b", t=PACK, b=8),
-                )
+            nc.vector.tensor_copy(
+                dealt[:].bitcast(I32).rearrange("p (t a m) -> p a t m", t=TILES, m=4),
+                picked[:].bitcast(I32).rearrange("p (a m t) -> p a t m", t=TILES, m=4),
+            )
             return dealt
 
-        def mx_pass(bank, t, lhs, lhs_plane, rhs, rhs_plane, first):
-            cols = slice(t * P, (t + 1) * P)
+        def deal_words_by_runs(picked, name):
+            dealt = work.tile([P, S], U32, name="dealt_" + name, align_bytes=64)
+            nc.vector.tensor_copy(
+                dealt[:].bitcast(I32).rearrange("p (t g b) -> p t g b", t=TILES, b=RUN),
+                picked[:].bitcast(I32).rearrange("p (g t b) -> p t g b", t=TILES, b=RUN),
+            )
+            return dealt
+
+        def mx_pass(bank, t, d_codes, d_plane, codes, plane, first):
+            tile_cols = slice(t * P, (t + 1) * P)
             nc.tensor.matmul_mx(
-                out=bank[:], lhsT=lhs[:, cols].bitcast(FP8X4), lhsT_scale=lhs_plane[:, cols],
-                rhs=rhs[:].bitcast(FP8X4), rhs_scale=rhs_plane, start=first, stop=not first,
+                out=bank[:], lhsT=d_codes[:, tile_cols].bitcast(FP8X4), lhsT_scale=d_plane[:, tile_cols],
+                rhs=codes.bitcast(FP8X4), rhs_scale=plane, start=first, stop=not first,
             )
 
-        def fetch_pairs(window, t, stage, first, second):
-            pair = work.tile([P, 2, W], F32, name="pair%d_%d" % (stage, t), tag="pair%d_%d" % (stage, t))
+        def fetch_pair(pair, window, first, second, second_on_vector=False):
             nc.scalar.activation(pair[:, 0, :], window[:].indirect(lists[first][:]), ACT.Copy)
-            if stage == 1 and t == 0:
+            if second_on_vector:
                 nc.vector.tensor_scalar(pair[:, 1, :], window[:].indirect(lists[second][:]), -1.0, 0.0, ALU.mult, ALU.add)
             else:
                 nc.scalar.activation(pair[:, 1, :], window[:].indirect(lists[second][:]), ACT.Copy, scale=-1.0)
-            return pair
 
-        def take_larger(pair, name, tag):
-            larger = work.tile([P, W], F32, name=name, tag=tag, align_bytes=64)
-            nc.vector.scalar_tensor_tensor(larger[:], pair[:, 1, :], -1.0, pair[:, 0, :], ALU.mult, ALU.max)
-            return larger
+        def take_larger(larger, first, negated):
+            nc.vector.scalar_tensor_tensor(larger, negated, -1.0, first, ALU.mult, ALU.max)
 
-        def place_difference(pair, name, tag, to_difference):
-            placed = work.tile([P, S], F32, name=name, tag=tag, align_bytes=64)
-            nc.vector.tensor_tensor(placed[:].indirect(lists[to_difference][:]), pair[:, 0, :], pair[:, 1, :], ALU.add)
-            return placed
+        def place_difference(placed, pair, name):
+            nc.vector.tensor_tensor(placed[:].indirect(lists[name][:]), pair[:, 0, :], pair[:, 1, :], ALU.add)
 
-        def place_larger(placed, larger, to_larger):
-            nc.vector.tensor_copy(placed[:].indirect(lists[to_larger][:]), larger[:])
+        def place_larger(placed, larger, name):
+            nc.vector.tensor_copy(placed[:].indirect(lists[name][:]), larger)
 
-        gather_scales(0, "picked_b0", "offs", ("ka", "kb"))
-        xq = gather_words(xw, "offs", "picked_offs")
-        da = deal_words(gather_words(dw, "ka", "picked_ka"), "ka")
-        db = deal_words(gather_words(dw, "kb", "picked_kb"), "kb")
+        gather_scales(0, "picked_bytes0", "offs", ("ka", "kb"), deal_bytes_by_fours)
+        x_offs = gather_words(x_word_window, "offs", "picked_offs")
+        d_ka = deal_words_by_fours(gather_words(d_word_window, "ka", "picked_ka"), "ka")
+        d_kb = deal_words_by_fours(gather_words(d_word_window, "kb", "picked_kb"), "kb")
 
-        banks = [psum.tile([P, S], F32, name="bank%d" % b) for b in range(2 * PACK)]
-        pairs = []
-        for t in range(PACK):
-            mx_pass(banks[t], t, da, planes[0][:, 1, :], xq, planes[0][:, 0, :], True)
-            mx_pass(banks[t], t, db, planes[0][:, 2, :], xq, planes[0][:, 0, :], False)
+        couples = [work.tile([P, 2, 2, W], F32, name="couple%d" % c) for c in range(2)]
+        for t in range(TILES):
+            bank = psum.tile([P, S], F32, name="h_bank%d" % t, tag="bank%d" % t)
+            mx_pass(bank, t, d_ka, planes[0][:, 1, :], x_offs[:], planes[0][:, 0, :], True)
+            mx_pass(bank, t, d_kb, planes[0][:, 2, :], x_offs[:], planes[0][:, 0, :], False)
             h = work.tile([P, S], F32, name="h%d" % t)
-            nc.scalar.activation(h[:], banks[t][:], ACT.Copy, scale=0.0625)
-            pairs.append(fetch_pairs(h, t, 0, "n1", "n2"))
+            nc.scalar.activation(h[:], bank[:], ACT.Copy, scale=SIXTEENTH)
+            fetch_pair(couples[t // 2][:, t % 2], h, "n1", "n2")
 
-        gather_scales(1, "picked_kb", "two", ("k1", "k2"))
-        x2 = gather_words(xw, "two", "picked_ka")
-        d2 = deal_words(gather_words(dw, "k2", "picked_k2"), "k2")
-        for t in range(PACK):
-            mx_pass(banks[PACK + t], t, d2, planes[1][:, 2, :], x2, planes[1][:, 0, :], True)
+        gather_scales(1, "picked_kb", "two", ("k1", "k2"), deal_bytes_by_runs)
+        x_two = gather_words(x_word_window, "two", "picked_ka")
+        d_k2 = deal_words_by_runs(gather_words(d_word_window, "k2", "picked_k2"), "k2")
 
-        for name, src, tag in (("sl", sl, "dealt_b0"), ("th", th, "picked_b0")):
-            cols4[name] = work.tile([P, PACK, 8], F32, name="row_" + name, tag=tag, align_bytes=64)
-            for t in range(PACK):
+        pieces = [(0, cols) for cols in HALVES] + [(t, slice(0, S)) for t in range(1, TILES)]
+        h2_banks = []
+        for n, (t, cols) in enumerate(pieces):
+            bank = psum.tile([P, cols.stop - cols.start], F32, name="h2_bank%d" % n, tag="bank%d" % ((TILES + n) % 8))
+            mx_pass(bank, t, d_k2, planes[1][:, 2, :], x_two[:, cols], planes[1][:, 0, cols], True)
+            h2_banks.append(bank)
+
+        by_row = {}
+        for name, src, tag in (("sl", sl, "dealt_bytes0"), ("th", th, "picked_bytes0")):
+            by_row[name] = work.tile([P, TILES, 8], F32, name="by_row_" + name, tag=tag, align_bytes=64)
+            for t in range(TILES):
                 with nc.allow_non_contiguous_dma(reason="one value a row"):
-                    nc.sync.dma_start(cols4[name][:, t, 0:1], src.rearrange("(g t b) o -> t g b o", t=PACK, b=8)[t])
-        bias = held.tile([P, PACK], F32, name="bias")
-        nc.vector.scalar_tensor_tensor(bias[:], cols4["sl"][:, :, 0], -1.0, cols4["th"][:, :, 0], ALU.mult, ALU.mult)
+                    nc.sync.dma_start(by_row[name][:, t, 0:1], src.rearrange("(g t b) o -> t g b o", t=TILES, b=RUN)[t])
+        bias = held.tile([P, TILES], F32, name="bias")
+        nc.vector.scalar_tensor_tensor(bias[:], by_row["sl"][:, :, 0], -1.0, by_row["th"][:, :, 0], ALU.mult, ALU.mult)
 
-        z_halves = [work.tile([P, W, PACK], BF16, name="z%d" % half, align_bytes=64) for half in range(2)]
-        for t in range(PACK):
-            larger = take_larger(pairs[t], "larger0_%d" % t, "larger0_%d" % t)
-            ub = place_difference(pairs[t], "ub%d" % t, "ub%d" % t, "n4")
-            place_larger(ub, larger, "n3")
-            for half in range(2):
-                nc.scalar.activation(
-                    z_halves[half][:, :, t], ub[:, half * W : (half + 1) * W], ACT.Copy, scale=cols4["gs"][:, t : t + 1]
-                )
+        z_halves = [work.tile([P, W, TILES], BF16, name="z%d" % half, align_bytes=64) for half in range(2)]
+        for c, couple in enumerate(couples):
+            larger = work.tile([P, 2, W], F32, name="larger_h%d" % c, tag="larger_h%d" % c, align_bytes=64)
+            take_larger(larger[:], couple[:, :, 0, :], couple[:, :, 1, :])
+            for u in range(2):
+                t = 2 * c + u
+                ub = work.tile([P, S], F32, name="ub%d" % t)
+                place_difference(ub, couple[:, u], "n4")
+                place_larger(ub, larger[:, u, :], "n3")
+                for half, cols in enumerate(HALVES):
+                    nc.scalar.activation(z_halves[half][:, :, t], ub[:, cols], ACT.Copy, scale=gains[:, t : t + 1])
 
-        d1 = deal_words(gather_words(dw, "k1", "larger0_3"), "k1")
+        d_k1 = deal_words_by_runs(gather_words(d_word_window, "k1", "larger_h1"), "k1")
         z_codes = work.tile([P, S], U32, name="z_codes", align_bytes=64)
         z_plane = work.tile([P, S], U8, name="z_plane", align_bytes=64)
-        for half in range(2):
-            cols = slice(half * W, (half + 1) * W)
+        for half, cols in enumerate(HALVES):
             nc.vector.quantize_mx(
                 out=z_codes[:, cols].bitcast(FP8X4), scales=z_plane[:, cols], in_=z_halves[half][:].rearrange("p c t -> p (c t)")
             )
 
-        def gate_rows(t):
-            bank = banks[PACK + t]
-            rows_t = slice(t * P, (t + 1) * P)
-            pieces = 2 if t == 0 else 1
-            width = S // pieces
-            for piece in range(pieces):
-                cols = slice(piece * width, (piece + 1) * width)
-                nc.tensor.matmul_mx(
-                    out=bank[:, cols], lhsT=d1[:, rows_t].bitcast(FP8X4), lhsT_scale=planes[1][:, 1, rows_t],
-                    rhs=z_codes[:, cols].bitcast(FP8X4), rhs_scale=z_plane[:, cols], start=False, stop=piece == pieces - 1,
-                )
+        def make_st(t):
+            early = t < 2
             h2 = work.tile([P, S], F32, name="h2_%d" % t, tag="h2_%d" % (t % 2))
-            if t < 2:
-                nc.vector.tensor_scalar(h2[:], bank[:], 0.0625, None, ALU.mult)
-            else:
-                nc.scalar.activation(h2[:], bank[:], ACT.Copy, scale=0.0625)
+            own = [(bank, cols) for bank, (owner, cols) in zip(h2_banks, pieces) if owner == t]
+            for bank, cols in own:
+                mx_pass(bank, t, d_k1, planes[1][:, 1, :], z_codes[:, cols], z_plane[:, cols], False)
+                if early:
+                    nc.vector.tensor_scalar(h2[:, cols], bank[:], SIXTEENTH, None, ALU.mult)
+                else:
+                    nc.scalar.activation(h2[:, cols], bank[:], ACT.Copy, scale=SIXTEENTH)
             sg = work.tile([P, S], F32, name="sg%d" % t, tag="sg%d" % t, align_bytes=64)
-            for half in range(2):
+            for half, cols in enumerate(HALVES):
                 nc.scalar.activation(
-                    sg[:, half * W : (half + 1) * W], h2[:].indirect(lists["n5"][:, half * 16 : (half + 1) * 16]), ACT.Sigmoid,
-                    scale=cols4["sl"][:, t, 0:1], bias=bias[:, t : t + 1],
+                    sg[:, cols], h2[:].indirect(lists["n5"][:, half * HALF_LIST : (half + 1) * HALF_LIST]), ACT.Sigmoid,
+                    scale=by_row["sl"][:, t, 0:1], bias=bias[:, t : t + 1],
                 )
-            st = work.tile([P, S], F32, name="st%d" % t, tag="st%d" % t if t < 2 else "pair1_%d" % (t - 2))
-            engine = nc.vector if t < 2 else nc.gpsimd
-            for piece in range(pieces):
-                cols = slice(piece * width, (piece + 1) * width)
+            st = work.tile([P, S], F32, name="st%d" % t, tag="st%d" % t if early else "pair%d" % (t - 2))
+            engine = nc.vector if early else nc.gpsimd
+            for bank, cols in own:
                 engine.tensor_tensor(st[:, cols], h2[:, cols], sg[:, cols], ALU.mult)
             return st
 
-        rows = out.rearrange("(g t b) c -> t g b c", t=PACK, b=8)
-        gated = [gate_rows(0)]
-        for t in range(PACK):
-            pair = fetch_pairs(gated[t], t, 1, "n6", "n7")
-            larger = take_larger(pair, "larger1_%d" % t, "larger1_%d" % t)
+        out_rows = out.rearrange("(g t b) c -> t g b c", t=TILES, b=RUN)
+        st_tiles = [make_st(0)]
+        for t in range(TILES):
+            pair = work.tile([P, 2, W], F32, name="pair%d" % t, tag="pair%d" % t)
+            fetch_pair(pair, st_tiles[t], "n6", "n7", second_on_vector=t == 0)
+            larger = work.tile([P, W], F32, name="larger_st%d" % t)
+            take_larger(larger[:], pair[:, 0, :], pair[:, 1, :])
             if t == 0:
-                gated.append(gate_rows(1))
-            result = place_difference(pair, "result%d" % t, "sg1" if t == 0 else "result%d" % t, "n9")
-            if t + 2 < PACK:
-                gated.append(gate_rows(t + 2))
-            place_larger(result, larger, "n8")
-            nc.sync.dma_start(rows[t], result[:])
+                st_tiles.append(make_st(1))
+            result = work.tile([P, S], F32, name="result%d" % t, tag="sg1" if t == 0 else "result%d" % t, align_bytes=64)
+            place_difference(result, pair, "n9")
+            if t + 2 < TILES:
+                st_tiles.append(make_st(t + 2))
+            place_larger(result, larger[:], "n8")
+            nc.sync.dma_start(out_rows[t], result[:])

from contextlib import ExitStack

import concourse.mybir as mybir

F32 = mybir.dt.float32
BF16 = mybir.dt.bfloat16
I32 = mybir.dt.int32
U32 = mybir.dt.uint32
U16 = mybir.dt.uint16
U8 = mybir.dt.uint8
FP8X4 = mybir.dt.float8_e4m3fn_x4
ACT = mybir.ActivationFunctionType
ALU = mybir.AluOpType

P = 128
TILES = 4
S = 512
W = 256
HALF_LIST = W // 16
RUN = 8
SCALE_ROWS = 16
SIXTEENTH = 0.0625
HALVES = (slice(0, W), slice(W, S))
FLOPS = 4 * 2 * 512 * 512 * 512


def tile_picked_ahzmtcpmxecpx_none_p_kernel(
    tc, x_words, x_scales, d_words, d_scales, gs, sl, th, offs, ka, kb, n1, n2, n3, n4, k1, k2, two, n5, n6, n7, n8, n9, out
):
    nc = tc.nc
    with ExitStack() as ctx:
        held = ctx.enter_context(tc.tile_pool(name="held", bufs=1))
        work = ctx.enter_context(tc.tile_pool(name="work", bufs=1))
        psum = ctx.enter_context(tc.psum_pool(name="psum", bufs=1))

        lists = {}
        for name, src in (
            ("offs", offs), ("ka", ka), ("kb", kb), ("n1", n1), ("n2", n2), ("two", two), ("k2", k2), ("k1", k1),
            ("n4", n4), ("n3", n3), ("n5", n5), ("n6", n6), ("n7", n7), ("n9", n9), ("n8", n8),
        ):
            lists[name] = held.tile(list(src.shape), U16, name="list_" + name)
            nc.sync.dma_start(lists[name][:], src)

        def load_scale_window(name, src):
            cols = src.shape[2]
            window = held.tile([P, cols], U8, name=name, align_bytes=64)
            scale_rows = src[0].bitcast(I32).unsqueeze(1).broadcast_to([SCALE_ROWS, P // SCALE_ROWS, cols // 4])
            nc.scalar.dma_start(window[:].bitcast(I32), scale_rows)
            return window

        def load_word_window(name, src):
            window = held.tile([P, src.shape[2]], U32, name=name, align_bytes=64)
            nc.scalar.dma_start(window[:].bitcast(I32), src[0].rearrange("p n t -> p (n t)").bitcast(I32))
            return window

        x_scale_window = load_scale_window("x_scale_window", x_scales)
        d_scale_window = load_scale_window("d_scale_window", d_scales)
        x_word_window = load_word_window("x_word_window", x_words)
        d_word_window = load_word_window("d_word_window", d_words)

        gains = held.tile([P, TILES], F32, name="gains")
        nc.sync.dma_start(gains[:], gs.rearrange("(p t) o -> p (t o)", t=TILES))

        planes = []
        for layer in range(2):
            plane = held.tile([P, 3, S], U8, name="planes%d" % layer, align_bytes=64)
            nc.vector.memset(plane[:].rearrange("p l c -> p (l c)").bitcast(I32), 0)
            planes.append(plane)

        def deal_bytes_by_fours(dealt, picked):
            nc.vector.tensor_copy(
                dealt.rearrange("p l (t a m) -> p l a t m", t=TILES, m=16),
                picked.rearrange("p l (a m t) -> p l a t m", t=TILES, m=16),
            )

        def deal_bytes_by_runs(dealt, picked):
            nc.vector.tensor_copy(
                dealt.bitcast(I32).rearrange("p l (t g b) -> p l t g b", t=TILES, b=RUN // 4),
                picked.bitcast(I32).rearrange("p l (g t b) -> p l t g b", t=TILES, b=RUN // 4),
            )

        def gather_scales(layer, tag, x_list, d_lists, deal):
            picked = work.tile([P, 3, S], U8, name="picked_bytes%d" % layer, tag=tag, align_bytes=64)
            nc.vector.tensor_copy(picked[:, 0, :], x_scale_window[:].indirect(lists[x_list][:]))
            for slot, name in enumerate(d_lists):
                nc.vector.tensor_copy(picked[:, 1 + slot, :], d_scale_window[:].indirect(lists[name][:]))
            dealt = work.tile([P, 2, S], U8, name="dealt_bytes%d" % layer, tag="dealt_bytes%d" % layer, align_bytes=64)
            deal(dealt[:], picked[:, 1:3, :])
            target = planes[layer][:].rearrange("p l c -> p (l c)").bitcast(I32)
            x_source = picked[:].rearrange("p l c -> p (l c)").bitcast(I32)
            d_source = dealt[:].rearrange("p l c -> p (l c)").bitcast(I32)
            for i in range(4):
                nc.sync.dma_start(target[i:P:32, 0 : S // 4], x_source[8 * i : P : 32, 0 : S // 4])
            for i in range(4):
                nc.sync.dma_start(target[i:P:32, S // 4 : 3 * S // 4], d_source[8 * i : P : 32, :])

        def gather_words(window, name, tag):
            picked = work.tile([P, S], U32, name="picked_" + name, tag=tag, align_bytes=64)
            nc.vector.tensor_copy(picked[:], window[:].indirect(lists[name][:]))
            return picked

        def deal_words_by_fours(picked, name):
            dealt = work.tile([P, S], U32, name="dealt_" + name, align_bytes=64)
            nc.vector.tensor_copy(
                dealt[:].bitcast(I32).rearrange("p (t a m) -> p a t m", t=TILES, m=4),
                picked[:].bitcast(I32).rearrange("p (a m t) -> p a t m", t=TILES, m=4),
            )
            return dealt

        def deal_words_by_runs(picked, name):
            dealt = work.tile([P, S], U32, name="dealt_" + name, align_bytes=64)
            nc.vector.tensor_copy(
                dealt[:].bitcast(I32).rearrange("p (t g b) -> p t g b", t=TILES, b=RUN),
                picked[:].bitcast(I32).rearrange("p (g t b) -> p t g b", t=TILES, b=RUN),
            )
            return dealt

        def mx_pass(bank, t, d_codes, d_plane, codes, plane, first):
            tile_cols = slice(t * P, (t + 1) * P)
            nc.tensor.matmul_mx(
                out=bank[:], lhsT=d_codes[:, tile_cols].bitcast(FP8X4), lhsT_scale=d_plane[:, tile_cols],
                rhs=codes.bitcast(FP8X4), rhs_scale=plane, start=first, stop=not first,
            )

        def fetch_pair(pair, window, first, second, second_on_vector=False):
            nc.scalar.activation(pair[:, 0, :], window[:].indirect(lists[first][:]), ACT.Copy)
            if second_on_vector:
                nc.vector.tensor_scalar(pair[:, 1, :], window[:].indirect(lists[second][:]), -1.0, 0.0, ALU.mult, ALU.add)
            else:
                nc.scalar.activation(pair[:, 1, :], window[:].indirect(lists[second][:]), ACT.Copy, scale=-1.0)

        def take_larger(larger, first, negated):
            nc.vector.scalar_tensor_tensor(larger, negated, -1.0, first, ALU.mult, ALU.max)

        def place_difference(placed, pair, name):
            nc.vector.tensor_tensor(placed[:].indirect(lists[name][:]), pair[:, 0, :], pair[:, 1, :], ALU.add)

        def place_larger(placed, larger, name):
            nc.vector.tensor_copy(placed[:].indirect(lists[name][:]), larger)

        gather_scales(0, "picked_bytes0", "offs", ("ka", "kb"), deal_bytes_by_fours)
        x_offs = gather_words(x_word_window, "offs", "picked_offs")
        d_ka = deal_words_by_fours(gather_words(d_word_window, "ka", "picked_ka"), "ka")
        d_kb = deal_words_by_fours(gather_words(d_word_window, "kb", "picked_kb"), "kb")

        couples = [work.tile([P, 2, 2, W], F32, name="couple%d" % c) for c in range(2)]
        for t in range(TILES):
            bank = psum.tile([P, S], F32, name="h_bank%d" % t, tag="bank%d" % t)
            mx_pass(bank, t, d_ka, planes[0][:, 1, :], x_offs[:], planes[0][:, 0, :], True)
            mx_pass(bank, t, d_kb, planes[0][:, 2, :], x_offs[:], planes[0][:, 0, :], False)
            h = work.tile([P, S], F32, name="h%d" % t)
            nc.scalar.activation(h[:], bank[:], ACT.Copy, scale=SIXTEENTH)
            fetch_pair(couples[t // 2][:, t % 2], h, "n1", "n2")

        gather_scales(1, "picked_kb", "two", ("k1", "k2"), deal_bytes_by_runs)
        x_two = gather_words(x_word_window, "two", "picked_ka")
        d_k2 = deal_words_by_runs(gather_words(d_word_window, "k2", "picked_k2"), "k2")

        pieces = [(0, cols) for cols in HALVES] + [(t, slice(0, S)) for t in range(1, TILES)]
        h2_banks = []
        for n, (t, cols) in enumerate(pieces):
            bank = psum.tile([P, cols.stop - cols.start], F32, name="h2_bank%d" % n, tag="bank%d" % ((TILES + n) % 8))
            mx_pass(bank, t, d_k2, planes[1][:, 2, :], x_two[:, cols], planes[1][:, 0, cols], True)
            h2_banks.append(bank)

        by_row = {}
        for name, src, tag in (("sl", sl, "dealt_bytes0"), ("th", th, "picked_bytes0")):
            by_row[name] = work.tile([P, TILES, 8], F32, name="by_row_" + name, tag=tag, align_bytes=64)
            for t in range(TILES):
                with nc.allow_non_contiguous_dma(reason="one value a row"):
                    nc.sync.dma_start(by_row[name][:, t, 0:1], src.rearrange("(g t b) o -> t g b o", t=TILES, b=RUN)[t])
        bias = held.tile([P, TILES], F32, name="bias")
        nc.vector.scalar_tensor_tensor(bias[:], by_row["sl"][:, :, 0], -1.0, by_row["th"][:, :, 0], ALU.mult, ALU.mult)

        z_halves = [work.tile([P, W, TILES], BF16, name="z%d" % half, align_bytes=64) for half in range(2)]
        for c, couple in enumerate(couples):
            larger = work.tile([P, 2, W], F32, name="larger_h%d" % c, tag="larger_h%d" % c, align_bytes=64)
            take_larger(larger[:], couple[:, :, 0, :], couple[:, :, 1, :])
            for u in range(2):
                t = 2 * c + u
                ub = work.tile([P, S], F32, name="ub%d" % t)
                place_difference(ub, couple[:, u], "n4")
                place_larger(ub, larger[:, u, :], "n3")
                for half, cols in enumerate(HALVES):
                    nc.scalar.activation(z_halves[half][:, :, t], ub[:, cols], ACT.Copy, scale=gains[:, t : t + 1])

        d_k1 = deal_words_by_runs(gather_words(d_word_window, "k1", "larger_h1"), "k1")
        z_codes = work.tile([P, S], U32, name="z_codes", align_bytes=64)
        z_plane = work.tile([P, S], U8, name="z_plane", align_bytes=64)
        for half, cols in enumerate(HALVES):
            nc.vector.quantize_mx(
                out=z_codes[:, cols].bitcast(FP8X4), scales=z_plane[:, cols], in_=z_halves[half][:].rearrange("p c t -> p (c t)")
            )

        def make_st(t):
            early = t < 2
            h2 = work.tile([P, S], F32, name="h2_%d" % t, tag="h2_%d" % (t % 2))
            own = [(bank, cols) for bank, (owner, cols) in zip(h2_banks, pieces) if owner == t]
            for bank, cols in own:
                mx_pass(bank, t, d_k1, planes[1][:, 1, :], z_codes[:, cols], z_plane[:, cols], False)
                if early:
                    nc.vector.tensor_scalar(h2[:, cols], bank[:], SIXTEENTH, None, ALU.mult)
                else:
                    nc.scalar.activation(h2[:, cols], bank[:], ACT.Copy, scale=SIXTEENTH)
            sg = work.tile([P, S], F32, name="sg%d" % t, tag="sg%d" % t, align_bytes=64)
            for half, cols in enumerate(HALVES):
                nc.scalar.activation(
                    sg[:, cols], h2[:].indirect(lists["n5"][:, half * HALF_LIST : (half + 1) * HALF_LIST]), ACT.Sigmoid,
                    scale=by_row["sl"][:, t, 0:1], bias=bias[:, t : t + 1],
                )
            st = work.tile([P, S], F32, name="st%d" % t, tag="st%d" % t if early else "pair%d" % (t - 2))
            engine = nc.vector if early else nc.gpsimd
            for bank, cols in own:
                engine.tensor_tensor(st[:, cols], h2[:, cols], sg[:, cols], ALU.mult)
            return st

        out_rows = out.rearrange("(g t b) c -> t g b c", t=TILES, b=RUN)
        st_tiles = [make_st(0)]
        for t in range(TILES):
            pair = work.tile([P, 2, W], F32, name="pair%d" % t, tag="pair%d" % t)
            fetch_pair(pair, st_tiles[t], "n6", "n7", second_on_vector=t == 0)
            larger = work.tile([P, W], F32, name="larger_st%d" % t)
            take_larger(larger[:], pair[:, 0, :], pair[:, 1, :])
            if t == 0:
                st_tiles.append(make_st(1))
            result = work.tile([P, S], F32, name="result%d" % t, tag="sg1" if t == 0 else "result%d" % t, align_bytes=64)
            place_difference(result, pair, "n9")
            if t + 2 < TILES:
                st_tiles.append(make_st(t + 2))
            place_larger(result, larger[:], "n8")
            nc.sync.dma_start(out_rows[t], result[:])
